import numpy as np
import ml_dtypes


def mxq(x, axis, fmt="e4m3"):
    dtype, down = {"e4m3": (ml_dtypes.float8_e4m3fn, 7), "e5m2": (ml_dtypes.float8_e5m2, 14)}[fmt]
    v = np.moveaxis(np.asarray(x, np.float32).astype(ml_dtypes.bfloat16).astype(np.float64), axis, -1)
    blocks = v.reshape(v.shape[:-1] + (-1, 32))
    amax = np.abs(blocks).max(-1, keepdims=True)
    byte = np.maximum(np.where(amax > 0, np.frexp(amax)[1] - 1 + 127, 0) - down, 1)
    scale = np.exp2(byte - 127.0)
    codes = (blocks / scale).astype(np.float32).astype(dtype).astype(np.float64)
    return np.moveaxis((codes * scale).reshape(v.shape), -1, axis)


WIDE = False


def mx_kscale(k):
    if not WIDE:
        return np.ones(k)
    levels = np.array([10, -10, 5, -5, 0])
    if k % 512:
        return np.exp2(np.random.permutation(np.resize(levels, k // 32))).repeat(32)
    a = np.empty((k // 512, 16))
    for p in range(k // 512):
        a[p, :8] = np.random.permutation(np.resize(levels, 8))
        for g in range(8):
            far = levels[np.abs(levels - a[p, g]) >= 10]
            a[p, g + 8] = far[np.random.randint(len(far))]
    return np.exp2(a.ravel()).repeat(32)


def f64(x):
    return np.asarray(x).astype(np.float64)


def striped(idx):
    return np.tile(idx.reshape(-1, 16).T, (8, 1)).astype(np.uint16)


def unstriped(offs):
    return offs[:16].T.reshape(-1).astype(np.int64)


def striped8(idx):
    return np.concatenate([x.reshape(-1, 16).T for x in idx]).astype(np.uint16)


def runs(offs, k):
    lists = np.stack([offs[16 * r : 16 * r + 16].T.reshape(-1) for r in range(8)]).astype(np.int64)
    return lists[np.arange(k) % 512 // 64]


def pack_weight(w):
    k, n = w.shape
    w = f64(np.asarray(w, np.float32).astype(ml_dtypes.bfloat16)).reshape(k // 32, 32, n)
    amax = np.abs(w).max(1)
    byte = np.clip(np.where(amax > 0, np.frexp(amax)[1] - 1 + 127 - 7, 1), 1, 254)
    scaled = (w * np.exp2(127.0 - byte)[:, None, :]).reshape(k, n).astype(np.float32)
    words = np.ascontiguousarray(scaled.reshape(k // 512, 128, 4, n).transpose(0, 1, 3, 2)).astype(ml_dtypes.float8_e4m3fn).view(np.uint8)
    return words, np.ascontiguousarray(byte.astype(np.uint8).reshape(k // 512, 16, n))


def unpack_weight(words, scales):
    g, p, n, _ = words.shape
    vals = np.ascontiguousarray(words).view(ml_dtypes.float8_e4m3fn).astype(np.float64) * np.repeat(np.exp2(scales.astype(np.float64) - 127.0), 8, axis=1)[..., None]
    return vals.transpose(0, 1, 3, 2).reshape(g * 512, n)


def sigmoid(v):
    return 1.0 / (1.0 + np.exp(-np.maximum(v, -700.0)))


K, T, S, G, H, W = 512, 1024, 512, 2048, 512, 256


def setup_inputs():
    n = np.random.standard_normal
    s = mx_kscale(K)[:, None]
    packed_xT = pack_weight(n((K, T)) * s)
    packed_dT = pack_weight(n((K, G)) / s)
    perm = np.stack([np.random.permutation(S) for _ in range(8)])
    return {
        "x_words": packed_xT[0],
        "x_scales": packed_xT[1],
        "d_words": packed_dT[0],
        "d_scales": packed_dT[1],
        "gs": (np.random.uniform(0.5, 1.5, (K, 1)) * s).astype(np.float32),
        "offs": striped(np.random.permutation(T)[:S]),
        "k1": striped8(np.random.randint(0, G, (8, H))),
        "n1": striped8(np.stack([np.random.permutation(S) for _ in range(8)])),
        "n2": striped8(np.stack([np.random.permutation(S) for _ in range(8)])),
        "k2": striped8(np.random.randint(0, G, (8, H))),
        "n3": striped8(perm[:, :W]),
        "n4": striped8(perm[:, W:]),
    }


def reference(x_words, x_scales, d_words, d_scales, gs, offs, k1, n1, n2, k2, n3, n4):
    d_k2 = unpack_weight(d_words, d_scales)[np.arange(K)[:, None], runs(k2, K)]
    d_k1 = unpack_weight(d_words, d_scales)[np.arange(K)[:, None], runs(k1, K)]
    xq = unpack_weight(x_words, x_scales)[:, unstriped(offs)]
    h = 0.0625 * (d_k1.T @ xq)
    st = h - (h[np.arange(H)[:, None], runs(n1, H)])
    z = f64(gs) * (st / (np.abs(st[np.arange(H)[:, None], runs(n2, H)]) + 0.5))
    h2 = 0.0625 * ((d_k2.T @ mxq(z, 0, "e4m3")))
    pb = h2[np.arange(H)[:, None], runs(n4, H)]
    pa = h2[np.arange(H)[:, None], runs(n3, H)]
    rb = pb * sigmoid(pb - pa)
    ra = pa * sigmoid(pa - pb)
    ds = np.zeros((H, S))
    ds[np.arange(H)[:, None], runs(n3, H)] = ra
    out = ds.copy()
    out[np.arange(H)[:, None], runs(n4, H)] = rb
    return out

@@ -1,0 +1,209 @@
+from contextlib import ExitStack
+
+import concourse.mybir as mybir
+
+K, T, S, G, W = 512, 1024, 512, 2048, 256
+FLOPS = 2 * 2 * 512 * 512 * 512
+
+F32 = mybir.dt.float32
+BF16 = mybir.dt.bfloat16
+I32 = mybir.dt.int32
+U32 = mybir.dt.uint32
+U16 = mybir.dt.uint16
+U8 = mybir.dt.uint8
+FP8X4 = mybir.dt.float8_e4m3fn_x4
+ACT = mybir.ActivationFunctionType
+ALU = mybir.AluOpType
+
+P = 128
+TILES = 4
+HALF = S // 2
+TINY = 2.0 ** -100
+
+
+def tile_picked_codehopnduel_none_p_kernel(
+    tc, x_words, x_scales, d_words, d_scales, gs, offs, k1, n1, n2, k2, n3, n4, out
+):
+    nc = tc.nc
+    with ExitStack() as ctx:
+        lists = ctx.enter_context(tc.tile_pool(name="lists", bufs=1))
+        held = ctx.enter_context(tc.tile_pool(name="held", bufs=1))
+        psum = ctx.enter_context(tc.psum_pool(name="psum", bufs=1))
+
+        def sbuf(name, cols, dtype):
+            return held.tile([P, cols], dtype, name=name, align_bytes=64)
+
+        def picked(name, dtype):
+            return held.tile([P, S], dtype, name=name, tag="picked", align_bytes=64)
+
+        def load_list(name, src):
+            tile = lists.tile([P, src.shape[1]], U16, name=name)
+            nc.sync.dma_start(tile[:], src)
+            return tile
+
+        def half_of(lst, b):
+            return lst[:, b * HALF // 16 : (b + 1) * HALF // 16]
+
+        def cols(b):
+            return slice(b * HALF, (b + 1) * HALF)
+
+        d_scale_table = sbuf("d_scale_table", G, U8)
+        x_scale_table = sbuf("x_scale_table", T, U8)
+        d_word_table = sbuf("d_word_table", G, I32)
+        x_word_table = sbuf("x_word_table", T, I32)
+        nc.gpsimd.memset(x_scale_table[:].bitcast(I32), 0)
+        k1_l = load_list("k1_l", k1)
+        d_rows = d_scales[0].bitcast(I32)
+        nc.sync.dma_start(d_scale_table[:].bitcast(I32), d_rows.unsqueeze(1).broadcast_to([16, 8, G // 4]))
+        offs_l = load_list("offs_l", offs)
+        nc.sync.dma_start(x_word_table[:], x_words[0].rearrange("p n t -> p (n t)").bitcast(I32))
+        nc.sync.dma_start(d_word_table[:], d_words[0].rearrange("p n t -> p (n t)").bitcast(I32))
+        x_rows = x_scales[0].bitcast(I32)
+        for s in range(4):
+            nc.scalar.dma_start(x_scale_table[:].bitcast(I32)[s:P:32, :], x_rows[s:16:4, :])
+        gain = sbuf("gain", TILES, F32)
+        nc.sync.dma_start(gain[:], gs.rearrange("(p t) o -> p (t o)", t=TILES))
+        k2_l = load_list("k2_l", k2)
+        n1_l = load_list("n1_l", n1)
+        n2_l = load_list("n2_l", n2)
+        n3_l = load_list("n3_l", n3)
+        n4_l = load_list("n4_l", n4)
+
+        def place_scale_rows(name, dealt):
+            placed = sbuf(name, S, U8)
+            nc.vector.tensor_copy(placed[:].bitcast(I32), dealt[:].bitcast(I32))
+            for s in range(1, 4):
+                nc.sync.dma_start(placed[:].bitcast(I32)[s:P:32, :], dealt[:].bitcast(I32)[8 * s : P : 32, :])
+            return placed
+
+        s1_picked = sbuf("s1_picked", S, U8)
+        nc.vector.tensor_copy(s1_picked[:], d_scale_table[:].indirect(k1_l[:]))
+        s1_dealt = sbuf("s1_dealt", S, U8)
+        nc.vector.tensor_copy(
+            s1_dealt[:].rearrange("p (t m) -> p t m", t=TILES), s1_picked[:].rearrange("p (m t) -> p t m", t=TILES)
+        )
+        s1 = place_scale_rows("s1", s1_dealt)
+        xw = sbuf("xw", S, U32)
+        nc.vector.tensor_copy(xw[:], x_word_table[:].bitcast(U32).indirect(offs_l[:]))
+        xs = sbuf("xs", S, U8)
+        nc.vector.tensor_copy(xs[:], x_scale_table[:].indirect(offs_l[:]))
+        w1_picked = picked("w1_picked", U32)
+        nc.vector.tensor_copy(w1_picked[:], d_word_table[:].bitcast(U32).indirect(k1_l[:]))
+        w1 = sbuf("w1", S, U32)
+        nc.vector.tensor_copy(
+            w1[:].bitcast(I32).rearrange("p (t c i) -> p c t i", t=TILES, i=4),
+            w1_picked[:].bitcast(I32).rearrange("p (c i t) -> p c t i", t=TILES, i=4),
+        )
+
+        neg_sign = sbuf("neg_sign", TILES, F32)
+        nc.scalar.activation(neg_sign[:], gain[:], ACT.Sign, scale=-1.0)
+        gain_size = sbuf("gain_size", TILES, F32)
+        nc.scalar.activation(gain_size[:], gain[:], ACT.Abs)
+        inv_root = sbuf("inv_root", TILES, F32)
+        nc.scalar.activation(inv_root[:], gain_size[:], ACT.Abs_reciprocal_sqrt, bias=TINY)
+        gain_root = sbuf("gain_root", TILES, F32)
+        nc.vector.scalar_tensor_tensor(gain_root[:], gain_size[:], 0.25, inv_root[:], ALU.mult, ALU.mult)
+
+        banks = [psum.tile([P, S], F32, name="bank%d" % b) for b in range(2 * TILES)]
+        first_order = (1, 0, 2, 3)
+        for t in first_order:
+            m = slice(t * P, (t + 1) * P)
+            nc.tensor.matmul_mx(banks[t][:], lhsT=w1[:, m].bitcast(FP8X4), lhsT_scale=s1[:, m],
+                                rhs=xw[:].bitcast(FP8X4), rhs_scale=xs[:], start=True, stop=True)
+
+        s2_picked = picked("s2_picked", U8)
+        nc.vector.tensor_copy(s2_picked[:], d_scale_table[:].indirect(k2_l[:]))
+        s2_dealt = sbuf("s2_dealt", S, U8)
+        nc.vector.tensor_copy(
+            s2_dealt[:].bitcast(I32).rearrange("p (t c) -> p t c", t=TILES),
+            s2_picked[:].bitcast(I32).rearrange("p (c t) -> p t c", t=TILES),
+        )
+        s2 = place_scale_rows("s2", s2_dealt)
+        w2_picked = picked("w2_picked", U32)
+        nc.vector.tensor_copy(w2_picked[:], d_word_table[:].bitcast(U32).indirect(k2_l[:]))
+        w2 = sbuf("w2", S, U32)
+        nc.vector.tensor_copy(
+            w2[:].bitcast(I32).rearrange("p (t c i) -> p c t i", t=TILES, i=4),
+            w2_picked[:].bitcast(I32).rearrange("p (c t i) -> p c t i", t=TILES, i=4),
+        )
+
+        h_table, h_plain = {}, {}
+        for t in first_order:
+            last = t == TILES - 1
+            h_table[t] = held.tile([P, S], F32, name="h_table%d" % t, tag="reuse0" if last else "h_table%d" % t, align_bytes=64)
+            h_plain[t] = held.tile([P, S], F32, name="h_plain%d" % t, tag="reuse1" if last else "h_plain%d" % t, align_bytes=64)
+            nc.scalar.activation(h_table[t][:], banks[t][:], ACT.Copy, scale=neg_sign[:, t : t + 1])
+            if t == 0:
+                nc.scalar.activation(h_plain[t][:], banks[t][:], ACT.Copy, scale=neg_sign[:, t : t + 1])
+            else:
+                nc.sync.dma_start(h_plain[t][:], h_table[t][:])
+        steps = []
+        for t in range(TILES):
+            step = sbuf("step%d" % t, S, F32)
+            for b in range(2):
+                nc.vector.tensor_tensor(step[:, cols(b)], h_table[t][:].indirect(half_of(n1_l, b)), h_plain[t][:, cols(b)], ALU.subtract)
+            steps.append(step)
+        z_f32 = [held.tile([P, TILES, HALF], F32, name="z_f32_%d" % b, tag="reuse%d" % b, align_bytes=64) for b in range(2)]
+        for t in range(TILES):
+            step = steps[t]
+            size = sbuf("size%d" % t, S, F32)
+            nc.scalar.activation(size[:], step[:], ACT.Abs, scale=0.0625)
+            root = sbuf("root%d" % t, S, F32)
+            nc.scalar.activation(root[:], size[:], ACT.Abs_reciprocal_sqrt, bias=0.5)
+            factor = sbuf("factor%d" % t, S, F32)
+            nc.scalar.activation(factor[:], root[:], ACT.Square, scale=gain_root[:, t : t + 1])
+            for b in range(2):
+                nc.vector.tensor_tensor(z_f32[b][:, t, :], factor[:].indirect(half_of(n2_l, b)), step[:, cols(b)], ALU.mult)
+
+        h2 = [sbuf("h2_%d" % t, S, F32) for t in range(TILES)]
+        z_bf = [sbuf("z_bf%d" % b, TILES * HALF, BF16) for b in range(2)]
+        for b, copy in ((0, nc.scalar.copy), (1, nc.vector.tensor_copy)):
+            copy(
+                z_bf[b][:].rearrange("p (c i t) -> p c t i", t=TILES, i=4),
+                z_f32[b][:].rearrange("p t (c i) -> p c t i", i=4),
+            )
+
+        def leave_bank(t, b):
+            nc.scalar.activation(h2[t][:, cols(b)], banks[b * TILES + t][:, 0:HALF], ACT.Copy, scale=0.0625)
+
+        for b in (1, 0):
+            zw = sbuf("zw%d" % b, HALF, U32)
+            zs = sbuf("zs%d" % b, HALF, U8)
+            nc.vector.quantize_mx(out=zw[:].bitcast(FP8X4), scales=zs[:], in_=z_bf[b][:])
+            for t in range(TILES):
+                m = slice(t * P, (t + 1) * P)
+                nc.tensor.matmul_mx(banks[b * TILES + t][:, 0:HALF], lhsT=w2[:, m].bitcast(FP8X4), lhsT_scale=s2[:, m],
+                                    rhs=zw[:].bitcast(FP8X4), rhs_scale=zs[:], start=True, stop=True)
+
+        out_rows = out.rearrange("(c t i) n -> t c i n", t=TILES, i=4)
+        pa = [sbuf("pa%d" % t, W, F32) for t in range(TILES)]
+        pb = [sbuf("pb%d" % t, W, F32) for t in range(TILES)]
+        lead = [sbuf("lead%d" % t, W, F32) for t in range(TILES)]
+        result = [sbuf("result%d" % t, S, F32) for t in range(TILES)]
+
+        def fetch_pairs(t):
+            if t == 0:
+                nc.vector.tensor_copy(pa[t][:], h2[t][:].indirect(n3_l[:]))
+            else:
+                nc.scalar.activation(pa[t][:], h2[t][:].indirect(n3_l[:]), ACT.Copy)
+            nc.scalar.activation(pb[t][:], h2[t][:].indirect(n4_l[:]), ACT.Copy)
+            nc.vector.tensor_tensor(lead[t][:], pa[t][:], pb[t][:], ALU.subtract)
+
+        def put_back(t, values, places, sign):
+            gate = sbuf("gate%d_%d" % (t, sign > 0), W, F32)
+            nc.scalar.activation(gate[:], lead[t][:], ACT.Sigmoid, scale=sign)
+            nc.vector.tensor_tensor(result[t][:].indirect(places[:]), values[:], gate[:], ALU.mult)
+
+        leave_bank(0, 1)
+        leave_bank(0, 0)
+        fetch_pairs(0)
+        put_back(0, pa[0], n3_l, 1.0)
+        for t in range(TILES):
+            if t + 1 < TILES:
+                leave_bank(t + 1, 1)
+                leave_bank(t + 1, 0)
+                fetch_pairs(t + 1)
+            put_back(t, pb[t], n4_l, -1.0)
+            nc.sync.dma_start(out_rows[t], result[t][:])
+            if t + 1 < TILES:
+                put_back(t + 1, pa[t + 1], n3_l, 1.0)

@@ -155,6 +155,9 @@ def tile_picked_codehopnduel_none_p_kernel(
             for b in range(2):
                 nc.vector.tensor_tensor(z_f32[b][:, t, :], factor[:].indirect(half_of(n2_l, b)), step[:, cols(b)], ALU.mult)
 
+        warm = sbuf("warm", 1, F32)
+        nc.scalar.activation(warm[:], factor[:, 0:1], ACT.Sigmoid)
+
         h2 = [sbuf("h2_%d" % t, S, F32) for t in range(TILES)]
         z_bf = [sbuf("z_bf%d" % b, TILES * HALF, BF16) for b in range(2)]
         for b, copy in ((0, nc.scalar.copy), (1, nc.vector.tensor_copy)):

@@ -28,13 +28,14 @@ def tile_picked_codehopnduel_none_p_kernel(
     with ExitStack() as ctx:
         lists = ctx.enter_context(tc.tile_pool(name="lists", bufs=1))
         held = ctx.enter_context(tc.tile_pool(name="held", bufs=1))
+        staging = ctx.enter_context(tc.tile_pool(name="staging", bufs=1))
         psum = ctx.enter_context(tc.psum_pool(name="psum", bufs=1))
 
         def sbuf(name, cols, dtype):
             return held.tile([P, cols], dtype, name=name, align_bytes=64)
 
-        def picked(name, dtype):
-            return held.tile([P, S], dtype, name=name, tag="picked", align_bytes=64)
+        def picked(name, dtype, offset):
+            return staging.tile([P, S], dtype, name=name, offset=offset, align_bytes=64)
 
         def load_list(name, src):
             tile = lists.tile([P, src.shape[1]], U16, name=name)
@@ -51,16 +52,18 @@ def tile_picked_codehopnduel_none_p_kernel(
         x_scale_table = sbuf("x_scale_table", T, U8)
         d_word_table = sbuf("d_word_table", G, I32)
         x_word_table = sbuf("x_word_table", T, I32)
-        nc.gpsimd.memset(x_scale_table[:].bitcast(I32), 0)
         k1_l = load_list("k1_l", k1)
         d_rows = d_scales[0].bitcast(I32)
         nc.sync.dma_start(d_scale_table[:].bitcast(I32), d_rows.unsqueeze(1).broadcast_to([16, 8, G // 4]))
-        offs_l = load_list("offs_l", offs)
-        nc.sync.dma_start(x_word_table[:], x_words[0].rearrange("p n t -> p (n t)").bitcast(I32))
-        nc.sync.dma_start(d_word_table[:], d_words[0].rearrange("p n t -> p (n t)").bitcast(I32))
         x_rows = x_scales[0].bitcast(I32)
-        for s in range(4):
-            nc.scalar.dma_start(x_scale_table[:].bitcast(I32)[s:P:32, :], x_rows[s:16:4, :])
+        for q in range(4):
+            nc.scalar.dma_start(
+                x_scale_table[:].bitcast(I32)[32 * q : 32 * q + 32, :],
+                x_rows[4 * q : 4 * q + 4, :].unsqueeze(0).broadcast_to([8, 4, T // 4]),
+            )
+        offs_l = load_list("offs_l", offs)
+        nc.sync.dma_start(d_word_table[:], d_words[0].rearrange("p n t -> p (n t)").bitcast(I32))
+        nc.sync.dma_start(x_word_table[:], x_words[0].rearrange("p n t -> p (n t)").bitcast(I32))
         gain = sbuf("gain", TILES, F32)
         nc.sync.dma_start(gain[:], gs.rearrange("(p t) o -> p (t o)", t=TILES))
         k2_l = load_list("k2_l", k2)
@@ -69,10 +72,10 @@ def tile_picked_codehopnduel_none_p_kernel(
         n3_l = load_list("n3_l", n3)
         n4_l = load_list("n4_l", n4)
 
-        def place_scale_rows(name, dealt):
-            placed = sbuf(name, S, U8)
-            nc.vector.tensor_copy(placed[:].bitcast(I32), dealt[:].bitcast(I32))
-            for s in range(1, 4):
+        def place_scale_rows(name, dealt, tag):
+            placed = held.tile([P, S], U8, name=name, tag=tag, align_bytes=64)
+            nc.gpsimd.memset(placed[:].bitcast(I32), 0)
+            for s in range(4):
                 nc.sync.dma_start(placed[:].bitcast(I32)[s:P:32, :], dealt[:].bitcast(I32)[8 * s : P : 32, :])
             return placed
 
@@ -82,13 +85,13 @@ def tile_picked_codehopnduel_none_p_kernel(
         nc.vector.tensor_copy(
             s1_dealt[:].rearrange("p (t m) -> p t m", t=TILES), s1_picked[:].rearrange("p (m t) -> p t m", t=TILES)
         )
-        s1 = place_scale_rows("s1", s1_dealt)
-        xw = sbuf("xw", S, U32)
-        nc.vector.tensor_copy(xw[:], x_word_table[:].bitcast(U32).indirect(offs_l[:]))
+        s1 = place_scale_rows("s1", s1_dealt, "s1")
         xs = sbuf("xs", S, U8)
         nc.vector.tensor_copy(xs[:], x_scale_table[:].indirect(offs_l[:]))
-        w1_picked = picked("w1_picked", U32)
+        w1_picked = picked("w1_picked", U32, 0)
         nc.vector.tensor_copy(w1_picked[:], d_word_table[:].bitcast(U32).indirect(k1_l[:]))
+        xw = sbuf("xw", S, U32)
+        nc.vector.tensor_copy(xw[:], x_word_table[:].bitcast(U32).indirect(offs_l[:]))
         w1 = sbuf("w1", S, U32)
         nc.vector.tensor_copy(
             w1[:].bitcast(I32).rearrange("p (t c i) -> p c t i", t=TILES, i=4),
@@ -100,113 +103,147 @@ def tile_picked_codehopnduel_none_p_kernel(
         gain_size = sbuf("gain_size", TILES, F32)
         nc.scalar.activation(gain_size[:], gain[:], ACT.Abs)
         inv_root = sbuf("inv_root", TILES, F32)
-        nc.scalar.activation(inv_root[:], gain_size[:], ACT.Abs_reciprocal_sqrt, bias=TINY)
+        nc.scalar.activation(inv_root[:], gain_size[:], ACT.Abs_reciprocal_sqrt, scale=16.0, bias=TINY)
         gain_root = sbuf("gain_root", TILES, F32)
-        nc.vector.scalar_tensor_tensor(gain_root[:], gain_size[:], 0.25, inv_root[:], ALU.mult, ALU.mult)
+        nc.gpsimd.tensor_tensor(gain_root[:], gain_size[:], inv_root[:], ALU.mult)
 
         banks = [psum.tile([P, S], F32, name="bank%d" % b) for b in range(2 * TILES)]
-        first_order = (1, 0, 2, 3)
+        first_order = (1, 2, 0, 3)
         for t in first_order:
             m = slice(t * P, (t + 1) * P)
             nc.tensor.matmul_mx(banks[t][:], lhsT=w1[:, m].bitcast(FP8X4), lhsT_scale=s1[:, m],
                                 rhs=xw[:].bitcast(FP8X4), rhs_scale=xs[:], start=True, stop=True)
 
-        s2_picked = picked("s2_picked", U8)
+        s2_picked = picked("s2_picked", U8, 0)
         nc.vector.tensor_copy(s2_picked[:], d_scale_table[:].indirect(k2_l[:]))
+        w2_picked = picked("w2_picked", U32, S)
+        nc.vector.tensor_copy(w2_picked[:], d_word_table[:].bitcast(U32).indirect(k2_l[:]))
         s2_dealt = sbuf("s2_dealt", S, U8)
         nc.vector.tensor_copy(
             s2_dealt[:].bitcast(I32).rearrange("p (t c) -> p t c", t=TILES),
             s2_picked[:].bitcast(I32).rearrange("p (c t) -> p t c", t=TILES),
         )
-        s2 = place_scale_rows("s2", s2_dealt)
-        w2_picked = picked("w2_picked", U32)
-        nc.vector.tensor_copy(w2_picked[:], d_word_table[:].bitcast(U32).indirect(k2_l[:]))
         w2 = sbuf("w2", S, U32)
         nc.vector.tensor_copy(
             w2[:].bitcast(I32).rearrange("p (t c i) -> p c t i", t=TILES, i=4),
             w2_picked[:].bitcast(I32).rearrange("p (c t i) -> p c t i", t=TILES, i=4),
         )
 
-        h_table, h_plain = {}, {}
+        wide = [sbuf("h_wide%d" % t, 2 * S if t else S, F32) for t in range(TILES)]
+        h_table = [wide[t][:, 0:S] for t in range(TILES)]
+        h_last = sbuf("h_last", S, F32)
+        h_plain = [wide[t + 1][:, S : 2 * S] for t in range(TILES - 1)] + [h_last[:]]
         for t in first_order:
-            last = t == TILES - 1
-            h_table[t] = held.tile([P, S], F32, name="h_table%d" % t, tag="reuse0" if last else "h_table%d" % t, align_bytes=64)
-            h_plain[t] = held.tile([P, S], F32, name="h_plain%d" % t, tag="reuse1" if last else "h_plain%d" % t, align_bytes=64)
-            nc.scalar.activation(h_table[t][:], banks[t][:], ACT.Copy, scale=neg_sign[:, t : t + 1])
+            nc.scalar.activation(h_table[t], banks[t][:], ACT.Copy, scale=neg_sign[:, t : t + 1])
             if t == 0:
-                nc.scalar.activation(h_plain[t][:], banks[t][:], ACT.Copy, scale=neg_sign[:, t : t + 1])
+                nc.scalar.activation(h_plain[t], banks[t][:], ACT.Copy, scale=neg_sign[:, t : t + 1])
             else:
-                nc.sync.dma_start(h_plain[t][:], h_table[t][:])
-        steps = []
-        for t in range(TILES):
-            step = sbuf("step%d" % t, S, F32)
-            for b in range(2):
-                nc.vector.tensor_tensor(step[:, cols(b)], h_table[t][:].indirect(half_of(n1_l, b)), h_plain[t][:, cols(b)], ALU.subtract)
-            steps.append(step)
-        z_f32 = [held.tile([P, TILES, HALF], F32, name="z_f32_%d" % b, tag="reuse%d" % b, align_bytes=64) for b in range(2)]
+                nc.sync.dma_start(h_plain[t], h_table[t])
+        steps = [sbuf("step%d" % t, S, F32) for t in range(TILES)]
+        for b in range(2):
+            nc.vector.tensor_tensor(steps[0][:, cols(b)], wide[0][:].indirect(half_of(n1_l, b)), h_plain[0][:, cols(b)], ALU.subtract)
+        for t in range(1, TILES):
+            nc.vector.tensor_tensor(steps[t][:], wide[t][:].indirect(n1_l[:]), h_plain[t], ALU.subtract)
+        s2 = place_scale_rows("s2", s2_dealt, "h_wide2")
+        z_f32 = held.tile([P, TILES, S], F32, name="z_f32", tag="h_last", align_bytes=64)
         for t in range(TILES):
             step = steps[t]
             size = sbuf("size%d" % t, S, F32)
-            nc.scalar.activation(size[:], step[:], ACT.Abs, scale=0.0625)
-            root = sbuf("root%d" % t, S, F32)
-            nc.scalar.activation(root[:], size[:], ACT.Abs_reciprocal_sqrt, bias=0.5)
-            factor = sbuf("factor%d" % t, S, F32)
-            nc.scalar.activation(factor[:], root[:], ACT.Square, scale=gain_root[:, t : t + 1])
+            both = sbuf("factor%d" % t, 2 * S, F32)
+            factor, root = both[:, 0:S], both[:, S : 2 * S]
             for b in range(2):
-                nc.vector.tensor_tensor(z_f32[b][:, t, :], factor[:].indirect(half_of(n2_l, b)), step[:, cols(b)], ALU.mult)
+                nc.scalar.activation(size[:, cols(b)], step[:, cols(b)], ACT.Abs, scale=0.0625)
+            for b in range(2):
+                nc.scalar.activation(root[:, cols(b)], size[:, cols(b)], ACT.Abs_reciprocal_sqrt, bias=0.5)
+            for b in range(2):
+                nc.scalar.activation(factor[:, cols(b)], root[:, cols(b)], ACT.Square, scale=gain_root[:, t : t + 1])
+            if t + 1 < TILES:
+                nc.vector.tensor_tensor(z_f32[:, t, :], both[:].indirect(n2_l[:]), step[:], ALU.mult)
+            else:
+                for b in range(2):
+                    nc.vector.tensor_tensor(z_f32[:, t, cols(b)], both[:].indirect(half_of(n2_l, b)), step[:, cols(b)], ALU.mult)
 
         warm = sbuf("warm", 1, F32)
-        nc.scalar.activation(warm[:], factor[:, 0:1], ACT.Sigmoid)
+        nc.scalar.activation(warm[:], factor[:, S - 1 : S], ACT.Sigmoid)
 
         h2 = [sbuf("h2_%d" % t, S, F32) for t in range(TILES)]
         z_bf = [sbuf("z_bf%d" % b, TILES * HALF, BF16) for b in range(2)]
-        for b, copy in ((0, nc.scalar.copy), (1, nc.vector.tensor_copy)):
+        for b, copy in ((0, nc.vector.tensor_copy), (1, nc.scalar.copy)):
             copy(
                 z_bf[b][:].rearrange("p (c i t) -> p c t i", t=TILES, i=4),
-                z_f32[b][:].rearrange("p t (c i) -> p c t i", i=4),
+                z_f32[:, :, cols(b)].rearrange("p t (c i) -> p c t i", i=4),
             )
 
-        def leave_bank(t, b):
-            nc.scalar.activation(h2[t][:, cols(b)], banks[b * TILES + t][:, 0:HALF], ACT.Copy, scale=0.0625)
+        zw = sbuf("zw", S, U32)
+        zs = sbuf("zs", S, U8)
 
-        for b in (1, 0):
-            zw = sbuf("zw%d" % b, HALF, U32)
-            zs = sbuf("zs%d" % b, HALF, U8)
-            nc.vector.quantize_mx(out=zw[:].bitcast(FP8X4), scales=zs[:], in_=z_bf[b][:])
-            for t in range(TILES):
-                m = slice(t * P, (t + 1) * P)
-                nc.tensor.matmul_mx(banks[b * TILES + t][:, 0:HALF], lhsT=w2[:, m].bitcast(FP8X4), lhsT_scale=s2[:, m],
-                                    rhs=zw[:].bitcast(FP8X4), rhs_scale=zs[:], start=True, stop=True)
+        def second_product(t, bank, span):
+            m = slice(t * P, (t + 1) * P)
+            nc.tensor.matmul_mx(bank[:, span], lhsT=w2[:, m].bitcast(FP8X4), lhsT_scale=s2[:, m],
+                                rhs=zw[:, span].bitcast(FP8X4), rhs_scale=zs[:, span], start=True, stop=True)
+            nc.scalar.activation(h2[t][:, span], bank[:, span], ACT.Copy, scale=0.0625)
+
+        for b in range(2):
+            nc.vector.quantize_mx(out=zw[:, cols(b)].bitcast(FP8X4), scales=zs[:, cols(b)], in_=z_bf[b][:])
+            second_product(0, banks[b], cols(b))
 
         out_rows = out.rearrange("(c t i) n -> t c i n", t=TILES, i=4)
-        pa = [sbuf("pa%d" % t, W, F32) for t in range(TILES)]
-        pb = [sbuf("pb%d" % t, W, F32) for t in range(TILES)]
-        lead = [sbuf("lead%d" % t, W, F32) for t in range(TILES)]
+        whole = slice(0, W)
+        early, late = slice(0, W // 2), slice(W // 2, W)
+        early_lead = held.tile([P, W // 2], F32, name="early_lead", tag="pairs1", align_bytes=64)
+        late_lead = sbuf("late_lead", W // 2, F32)
+        gate_a = [sbuf("gate_a%d" % t, W, F32) for t in range(TILES)]
+        early_gate_b = sbuf("early_gate_b", W // 2, F32)
         result = [sbuf("result%d" % t, S, F32) for t in range(TILES)]
 
-        def fetch_pairs(t):
-            if t == 0:
-                nc.vector.tensor_copy(pa[t][:], h2[t][:].indirect(n3_l[:]))
-            else:
-                nc.scalar.activation(pa[t][:], h2[t][:].indirect(n3_l[:]), ACT.Copy)
-            nc.scalar.activation(pb[t][:], h2[t][:].indirect(n4_l[:]), ACT.Copy)
-            nc.vector.tensor_tensor(lead[t][:], pa[t][:], pb[t][:], ALU.subtract)
+        def entries(lst, span):
+            return lst[:, span.start // 16 : span.stop // 16]
 
-        def put_back(t, values, places, sign):
-            gate = sbuf("gate%d_%d" % (t, sign > 0), W, F32)
-            nc.scalar.activation(gate[:], lead[t][:], ACT.Sigmoid, scale=sign)
-            nc.vector.tensor_tensor(result[t][:].indirect(places[:]), values[:], gate[:], ALU.mult)
+        def fetch(engine_copy, values, t, places, span):
+            engine_copy(values[:, span], h2[t][:].indirect(entries(places, span)))
 
-        leave_bank(0, 1)
-        leave_bank(0, 0)
-        fetch_pairs(0)
-        put_back(0, pa[0], n3_l, 1.0)
+        def scalar_copy(dst, src):
+            nc.scalar.activation(dst, src, ACT.Copy)
+
+        def gate(dst, lead, sign):
+            nc.scalar.activation(dst, lead, ACT.Sigmoid, scale=sign)
+
+        def put_back(t, values, gates, places, span):
+            nc.vector.tensor_tensor(result[t][:].indirect(entries(places, span)), values[:, span], gates, ALU.mult)
+
+        pairs = sbuf("pairs0", 2 * W, F32)
+        pa, pb = pairs[:, 0:W], pairs[:, W : 2 * W]
+        for span in (early, late):
+            fetch(nc.vector.tensor_copy, pa, 0, n3_l, span)
+            fetch(scalar_copy, pb, 0, n4_l, span)
+        for span, lead in ((early, early_lead), (late, late_lead)):
+            nc.vector.tensor_tensor(lead[:], pa[:, span], pb[:, span], ALU.subtract)
+        gate(gate_a[0][:, early], early_lead[:], 1.0)
+        put_back(0, pa, gate_a[0][:, early], n3_l, early)
+        gate(early_gate_b[:], early_lead[:], -1.0)
+        put_back(0, pb, early_gate_b[:], n4_l, early)
+        gate(gate_a[0][:, late], late_lead[:], 1.0)
+        put_back(0, pa, gate_a[0][:, late], n3_l, late)
+        second_product(1, banks[TILES], slice(0, S))
+        owed_lead, owed = late_lead, late
         for t in range(TILES):
-            if t + 1 < TILES:
-                leave_bank(t + 1, 1)
-                leave_bank(t + 1, 0)
-                fetch_pairs(t + 1)
-            put_back(t, pb[t], n4_l, -1.0)
+            more = t + 1 < TILES
+            if more:
+                pairs = sbuf("pairs%d" % (t + 1), 2 * W, F32)
+                next_pa, next_pb = pairs[:, 0:W], pairs[:, W : 2 * W]
+                fetch(scalar_copy, next_pa, t + 1, n3_l, whole)
+                fetch(scalar_copy, next_pb, t + 1, n4_l, whole)
+                lead = sbuf("lead%d" % (t + 1), W, F32)
+                nc.vector.tensor_tensor(lead[:], next_pa, next_pb, ALU.subtract)
+            gate_b = held.tile([P, owed.stop - owed.start], F32, name="gate_b%d" % t,
+                               tag="h2_%d" % (t + 1) if more else "gate_b_last", align_bytes=64)
+            gate(gate_b[:], owed_lead[:], -1.0)
+            put_back(t, pb, gate_b[:], n4_l, owed)
             nc.sync.dma_start(out_rows[t], result[t][:])
-            if t + 1 < TILES:
-                put_back(t + 1, pa[t + 1], n3_l, 1.0)
+            if t + 2 < TILES:
+                second_product(t + 2, banks[TILES], slice(0, S))
+            if more:
+                pa, pb = next_pa, next_pb
+                gate(gate_a[t + 1][:], lead[:], 1.0)
+                put_back(t + 1, pa, gate_a[t + 1][:], n3_l, whole)
+                owed_lead, owed = lead, whole

@@ -54,16 +54,16 @@ def tile_picked_codehopnduel_none_p_kernel(
         x_word_table = sbuf("x_word_table", T, I32)
         k1_l = load_list("k1_l", k1)
         d_rows = d_scales[0].bitcast(I32)
-        nc.sync.dma_start(d_scale_table[:].bitcast(I32), d_rows.unsqueeze(1).broadcast_to([16, 8, G // 4]))
+        nc.scalar.dma_start(d_scale_table[:].bitcast(I32), d_rows.unsqueeze(1).broadcast_to([16, 8, G // 4]))
+        nc.scalar.dma_start(d_word_table[:], d_words[0].rearrange("p n t -> p (n t)").bitcast(I32))
+        nc.scalar.dma_start(x_word_table[:], x_words[0].rearrange("p n t -> p (n t)").bitcast(I32))
+        offs_l = load_list("offs_l", offs)
         x_rows = x_scales[0].bitcast(I32)
         for q in range(4):
-            nc.scalar.dma_start(
+            nc.sync.dma_start(
                 x_scale_table[:].bitcast(I32)[32 * q : 32 * q + 32, :],
                 x_rows[4 * q : 4 * q + 4, :].unsqueeze(0).broadcast_to([8, 4, T // 4]),
             )
-        offs_l = load_list("offs_l", offs)
-        nc.sync.dma_start(d_word_table[:], d_words[0].rearrange("p n t -> p (n t)").bitcast(I32))
-        nc.sync.dma_start(x_word_table[:], x_words[0].rearrange("p n t -> p (n t)").bitcast(I32))
         gain = sbuf("gain", TILES, F32)
         nc.sync.dma_start(gain[:], gs.rearrange("(p t) o -> p (t o)", t=TILES))
         k2_l = load_list("k2_l", k2)
@@ -167,11 +167,14 @@ def tile_picked_codehopnduel_none_p_kernel(
         nc.scalar.activation(warm[:], factor[:, S - 1 : S], ACT.Sigmoid)
 
         h2 = [sbuf("h2_%d" % t, S, F32) for t in range(TILES)]
-        z_bf = [sbuf("z_bf%d" % b, TILES * HALF, BF16) for b in range(2)]
-        for b, copy in ((0, nc.vector.tensor_copy), (1, nc.scalar.copy)):
+        pieces = (slice(0, HALF), slice(HALF, HALF + P), slice(HALF + P, S))
+        z_bf = []
+        for n, span in enumerate(pieces):
+            z_bf.append(sbuf("z_bf%d" % n, TILES * (span.stop - span.start), BF16))
+            copy = nc.scalar.copy if n else nc.vector.tensor_copy
             copy(
-                z_bf[b][:].rearrange("p (c i t) -> p c t i", t=TILES, i=4),
-                z_f32[:, :, cols(b)].rearrange("p t (c i) -> p c t i", i=4),
+                z_bf[n][:].rearrange("p (c i t) -> p c t i", t=TILES, i=4),
+                z_f32[:, :, span].rearrange("p t (c i) -> p c t i", i=4),
             )
 
         zw = sbuf("zw", S, U32)
@@ -183,9 +186,9 @@ def tile_picked_codehopnduel_none_p_kernel(
                                 rhs=zw[:, span].bitcast(FP8X4), rhs_scale=zs[:, span], start=True, stop=True)
             nc.scalar.activation(h2[t][:, span], bank[:, span], ACT.Copy, scale=0.0625)
 
-        for b in range(2):
-            nc.vector.quantize_mx(out=zw[:, cols(b)].bitcast(FP8X4), scales=zs[:, cols(b)], in_=z_bf[b][:])
-            second_product(0, banks[b], cols(b))
+        for n, span in enumerate(pieces):
+            nc.vector.quantize_mx(out=zw[:, span].bitcast(FP8X4), scales=zs[:, span], in_=z_bf[n][:])
+            second_product(0, banks[n], span)
 
         out_rows = out.rearrange("(c t i) n -> t c i n", t=TILES, i=4)
         whole = slice(0, W)

from contextlib import ExitStack

import concourse.mybir as mybir

K, T, S, G, W = 512, 1024, 512, 2048, 256
FLOPS = 2 * 2 * 512 * 512 * 512

F32 = mybir.dt.float32
BF16 = mybir.dt.bfloat16
I32 = mybir.dt.int32
U32 = mybir.dt.uint32
U16 = mybir.dt.uint16
U8 = mybir.dt.uint8
FP8X4 = mybir.dt.float8_e4m3fn_x4
ACT = mybir.ActivationFunctionType
ALU = mybir.AluOpType

P = 128
TILES = 4
HALF = S // 2
TINY = 2.0 ** -100


def tile_picked_codehopnduel_none_p_kernel(
    tc, x_words, x_scales, d_words, d_scales, gs, offs, k1, n1, n2, k2, n3, n4, out
):
    nc = tc.nc
    with ExitStack() as ctx:
        lists = ctx.enter_context(tc.tile_pool(name="lists", bufs=1))
        held = ctx.enter_context(tc.tile_pool(name="held", bufs=1))
        staging = ctx.enter_context(tc.tile_pool(name="staging", bufs=1))
        psum = ctx.enter_context(tc.psum_pool(name="psum", bufs=1))

        def sbuf(name, cols, dtype):
            return held.tile([P, cols], dtype, name=name, align_bytes=64)

        def picked(name, dtype, offset):
            return staging.tile([P, S], dtype, name=name, offset=offset, align_bytes=64)

        def load_list(name, src):
            tile = lists.tile([P, src.shape[1]], U16, name=name)
            nc.sync.dma_start(tile[:], src)
            return tile

        def half_of(lst, b):
            return lst[:, b * HALF // 16 : (b + 1) * HALF // 16]

        def cols(b):
            return slice(b * HALF, (b + 1) * HALF)

        d_scale_table = sbuf("d_scale_table", G, U8)
        x_scale_table = sbuf("x_scale_table", T, U8)
        d_word_table = sbuf("d_word_table", G, I32)
        x_word_table = sbuf("x_word_table", T, I32)
        k1_l = load_list("k1_l", k1)
        d_rows = d_scales[0].bitcast(I32)
        nc.scalar.dma_start(d_scale_table[:].bitcast(I32), d_rows.unsqueeze(1).broadcast_to([16, 8, G // 4]))
        nc.scalar.dma_start(d_word_table[:], d_words[0].rearrange("p n t -> p (n t)").bitcast(I32))
        nc.scalar.dma_start(x_word_table[:], x_words[0].rearrange("p n t -> p (n t)").bitcast(I32))
        offs_l = load_list("offs_l", offs)
        x_rows = x_scales[0].bitcast(I32)
        for q in range(4):
            nc.sync.dma_start(
                x_scale_table[:].bitcast(I32)[32 * q : 32 * q + 32, :],
                x_rows[4 * q : 4 * q + 4, :].unsqueeze(0).broadcast_to([8, 4, T // 4]),
            )
        gain = sbuf("gain", TILES, F32)
        nc.sync.dma_start(gain[:], gs.rearrange("(p t) o -> p (t o)", t=TILES))
        k2_l = load_list("k2_l", k2)
        n1_l = load_list("n1_l", n1)
        n2_l = load_list("n2_l", n2)
        n3_l = load_list("n3_l", n3)
        n4_l = load_list("n4_l", n4)

        def place_scale_rows(name, dealt, tag):
            placed = held.tile([P, S], U8, name=name, tag=tag, align_bytes=64)
            nc.gpsimd.memset(placed[:].bitcast(I32), 0)
            for s in range(4):
                nc.sync.dma_start(placed[:].bitcast(I32)[s:P:32, :], dealt[:].bitcast(I32)[8 * s : P : 32, :])
            return placed

        s1_picked = sbuf("s1_picked", S, U8)
        nc.vector.tensor_copy(s1_picked[:], d_scale_table[:].indirect(k1_l[:]))
        s1_dealt = sbuf("s1_dealt", S, U8)
        nc.vector.tensor_copy(
            s1_dealt[:].rearrange("p (t m) -> p t m", t=TILES), s1_picked[:].rearrange("p (m t) -> p t m", t=TILES)
        )
        s1 = place_scale_rows("s1", s1_dealt, "s1")
        xs = sbuf("xs", S, U8)
        nc.vector.tensor_copy(xs[:], x_scale_table[:].indirect(offs_l[:]))
        w1_picked = picked("w1_picked", U32, 0)
        nc.vector.tensor_copy(w1_picked[:], d_word_table[:].bitcast(U32).indirect(k1_l[:]))
        xw = sbuf("xw", S, U32)
        nc.vector.tensor_copy(xw[:], x_word_table[:].bitcast(U32).indirect(offs_l[:]))
        w1 = sbuf("w1", S, U32)
        nc.vector.tensor_copy(
            w1[:].bitcast(I32).rearrange("p (t c i) -> p c t i", t=TILES, i=4),
            w1_picked[:].bitcast(I32).rearrange("p (c i t) -> p c t i", t=TILES, i=4),
        )

        neg_sign = sbuf("neg_sign", TILES, F32)
        nc.scalar.activation(neg_sign[:], gain[:], ACT.Sign, scale=-1.0)
        gain_size = sbuf("gain_size", TILES, F32)
        nc.scalar.activation(gain_size[:], gain[:], ACT.Abs)
        inv_root = sbuf("inv_root", TILES, F32)
        nc.scalar.activation(inv_root[:], gain_size[:], ACT.Abs_reciprocal_sqrt, scale=16.0, bias=TINY)
        gain_root = sbuf("gain_root", TILES, F32)
        nc.gpsimd.tensor_tensor(gain_root[:], gain_size[:], inv_root[:], ALU.mult)

        banks = [psum.tile([P, S], F32, name="bank%d" % b) for b in range(2 * TILES)]
        first_order = (1, 2, 0, 3)
        for t in first_order:
            m = slice(t * P, (t + 1) * P)
            nc.tensor.matmul_mx(banks[t][:], lhsT=w1[:, m].bitcast(FP8X4), lhsT_scale=s1[:, m],
                                rhs=xw[:].bitcast(FP8X4), rhs_scale=xs[:], start=True, stop=True)

        s2_picked = picked("s2_picked", U8, 0)
        nc.vector.tensor_copy(s2_picked[:], d_scale_table[:].indirect(k2_l[:]))
        w2_picked = picked("w2_picked", U32, S)
        nc.vector.tensor_copy(w2_picked[:], d_word_table[:].bitcast(U32).indirect(k2_l[:]))
        s2_dealt = sbuf("s2_dealt", S, U8)
        nc.vector.tensor_copy(
            s2_dealt[:].bitcast(I32).rearrange("p (t c) -> p t c", t=TILES),
            s2_picked[:].bitcast(I32).rearrange("p (c t) -> p t c", t=TILES),
        )
        w2 = sbuf("w2", S, U32)
        nc.vector.tensor_copy(
            w2[:].bitcast(I32).rearrange("p (t c i) -> p c t i", t=TILES, i=4),
            w2_picked[:].bitcast(I32).rearrange("p (c t i) -> p c t i", t=TILES, i=4),
        )

        wide = [sbuf("h_wide%d" % t, 2 * S if t else S, F32) for t in range(TILES)]
        h_table = [wide[t][:, 0:S] for t in range(TILES)]
        h_last = sbuf("h_last", S, F32)
        h_plain = [wide[t + 1][:, S : 2 * S] for t in range(TILES - 1)] + [h_last[:]]
        for t in first_order:
            nc.scalar.activation(h_table[t], banks[t][:], ACT.Copy, scale=neg_sign[:, t : t + 1])
            if t == 0:
                nc.scalar.activation(h_plain[t], banks[t][:], ACT.Copy, scale=neg_sign[:, t : t + 1])
            else:
                nc.sync.dma_start(h_plain[t], h_table[t])
        steps = [sbuf("step%d" % t, S, F32) for t in range(TILES)]
        for b in range(2):
            nc.vector.tensor_tensor(steps[0][:, cols(b)], wide[0][:].indirect(half_of(n1_l, b)), h_plain[0][:, cols(b)], ALU.subtract)
        for t in range(1, TILES):
            nc.vector.tensor_tensor(steps[t][:], wide[t][:].indirect(n1_l[:]), h_plain[t], ALU.subtract)
        s2 = place_scale_rows("s2", s2_dealt, "h_wide2")
        z_f32 = held.tile([P, TILES, S], F32, name="z_f32", tag="h_last", align_bytes=64)
        for t in range(TILES):
            step = steps[t]
            size = sbuf("size%d" % t, S, F32)
            both = sbuf("factor%d" % t, 2 * S, F32)
            factor, root = both[:, 0:S], both[:, S : 2 * S]
            for b in range(2):
                nc.scalar.activation(size[:, cols(b)], step[:, cols(b)], ACT.Abs, scale=0.0625)
            for b in range(2):
                nc.scalar.activation(root[:, cols(b)], size[:, cols(b)], ACT.Abs_reciprocal_sqrt, bias=0.5)
            for b in range(2):
                nc.scalar.activation(factor[:, cols(b)], root[:, cols(b)], ACT.Square, scale=gain_root[:, t : t + 1])
            if t + 1 < TILES:
                nc.vector.tensor_tensor(z_f32[:, t, :], both[:].indirect(n2_l[:]), step[:], ALU.mult)
            else:
                for b in range(2):
                    nc.vector.tensor_tensor(z_f32[:, t, cols(b)], both[:].indirect(half_of(n2_l, b)), step[:, cols(b)], ALU.mult)

        warm = sbuf("warm", 1, F32)
        nc.scalar.activation(warm[:], factor[:, S - 1 : S], ACT.Sigmoid)

        h2 = [sbuf("h2_%d" % t, S, F32) for t in range(TILES)]
        pieces = (slice(0, HALF), slice(HALF, HALF + P), slice(HALF + P, S))
        z_bf = []
        for n, span in enumerate(pieces):
            z_bf.append(sbuf("z_bf%d" % n, TILES * (span.stop - span.start), BF16))
            copy = nc.scalar.copy if n else nc.vector.tensor_copy
            copy(
                z_bf[n][:].rearrange("p (c i t) -> p c t i", t=TILES, i=4),
                z_f32[:, :, span].rearrange("p t (c i) -> p c t i", i=4),
            )

        zw = sbuf("zw", S, U32)
        zs = sbuf("zs", S, U8)

        def second_product(t, bank, span):
            m = slice(t * P, (t + 1) * P)
            nc.tensor.matmul_mx(bank[:, span], lhsT=w2[:, m].bitcast(FP8X4), lhsT_scale=s2[:, m],
                                rhs=zw[:, span].bitcast(FP8X4), rhs_scale=zs[:, span], start=True, stop=True)
            nc.scalar.activation(h2[t][:, span], bank[:, span], ACT.Copy, scale=0.0625)

        for n, span in enumerate(pieces):
            nc.vector.quantize_mx(out=zw[:, span].bitcast(FP8X4), scales=zs[:, span], in_=z_bf[n][:])
            second_product(0, banks[n], span)

        out_rows = out.rearrange("(c t i) n -> t c i n", t=TILES, i=4)
        whole = slice(0, W)
        early, late = slice(0, W // 2), slice(W // 2, W)
        early_lead = held.tile([P, W // 2], F32, name="early_lead", tag="pairs1", align_bytes=64)
        late_lead = sbuf("late_lead", W // 2, F32)
        gate_a = [sbuf("gate_a%d" % t, W, F32) for t in range(TILES)]
        early_gate_b = sbuf("early_gate_b", W // 2, F32)
        result = [sbuf("result%d" % t, S, F32) for t in range(TILES)]

        def entries(lst, span):
            return lst[:, span.start // 16 : span.stop // 16]

        def fetch(engine_copy, values, t, places, span):
            engine_copy(values[:, span], h2[t][:].indirect(entries(places, span)))

        def scalar_copy(dst, src):
            nc.scalar.activation(dst, src, ACT.Copy)

        def gate(dst, lead, sign):
            nc.scalar.activation(dst, lead, ACT.Sigmoid, scale=sign)

        def put_back(t, values, gates, places, span):
            nc.vector.tensor_tensor(result[t][:].indirect(entries(places, span)), values[:, span], gates, ALU.mult)

        pairs = sbuf("pairs0", 2 * W, F32)
        pa, pb = pairs[:, 0:W], pairs[:, W : 2 * W]
        for span in (early, late):
            fetch(nc.vector.tensor_copy, pa, 0, n3_l, span)
            fetch(scalar_copy, pb, 0, n4_l, span)
        for span, lead in ((early, early_lead), (late, late_lead)):
            nc.vector.tensor_tensor(lead[:], pa[:, span], pb[:, span], ALU.subtract)
        gate(gate_a[0][:, early], early_lead[:], 1.0)
        put_back(0, pa, gate_a[0][:, early], n3_l, early)
        gate(early_gate_b[:], early_lead[:], -1.0)
        put_back(0, pb, early_gate_b[:], n4_l, early)
        gate(gate_a[0][:, late], late_lead[:], 1.0)
        put_back(0, pa, gate_a[0][:, late], n3_l, late)
        second_product(1, banks[TILES], slice(0, S))
        owed_lead, owed = late_lead, late
        for t in range(TILES):
            more = t + 1 < TILES
            if more:
                pairs = sbuf("pairs%d" % (t + 1), 2 * W, F32)
                next_pa, next_pb = pairs[:, 0:W], pairs[:, W : 2 * W]
                fetch(scalar_copy, next_pa, t + 1, n3_l, whole)
                fetch(scalar_copy, next_pb, t + 1, n4_l, whole)
                lead = sbuf("lead%d" % (t + 1), W, F32)
                nc.vector.tensor_tensor(lead[:], next_pa, next_pb, ALU.subtract)
            gate_b = held.tile([P, owed.stop - owed.start], F32, name="gate_b%d" % t,
                               tag="h2_%d" % (t + 1) if more else "gate_b_last", align_bytes=64)
            gate(gate_b[:], owed_lead[:], -1.0)
            put_back(t, pb, gate_b[:], n4_l, owed)
            nc.sync.dma_start(out_rows[t], result[t][:])
            if t + 2 < TILES:
                second_product(t + 2, banks[TILES], slice(0, S))
            if more:
                pa, pb = next_pa, next_pb
                gate(gate_a[t + 1][:], lead[:], 1.0)
                put_back(t + 1, pa, gate_a[t + 1][:], n3_l, whole)
                owed_lead, owed = lead, whole
